import numpy as np
CORES = [0,7,8,15,16,23,24,31,32,39,40,47,48,55,56,63]
N = 16
GROUPS = [[0,1],[2,3],[4,5],[6,7],[8,9],[10,11],[12,13],[14,15]]
def setup_inputs(rng):
    return {"x": rng.standard_normal((N, 128, 128), dtype=np.float32)}
def reference(x):
    y = np.empty((N, 128, 128), x.dtype)
    for g in GROUPS:
        s = x[g].sum(axis=0, dtype=np.float64).astype(x[g].dtype)
        for r in g:
            y[r] = s
    return {"y": y}

from concourse.mybir import AluOpType

SCRATCH = {
    "mine": ("sbuf", [128, 128], "float32"),
    "land": ("sbuf", [128, 128], "float32"),
}
SEMAPHORES = ["loaded", "seeded", "sent", "arrived", "stored"]


def rank_program(g, core, T, topo):
    rank = T.rank_of(core)
    if rank is None:
        return

    group = [grp for grp in T.tables["GROUPS"] if rank in grp][0]
    peer = [T.cores[r] for r in group if r != rank][0]
    rid, pid, _se = topo.addr(peer)
    mask = topo.mask(core, peer)
    n_eng = bin(mask).count("1")

    g.sync.dma_start(T.mine[:], T.x[:]).then_inc(T.sem.loaded, 16)
    g.scalar.dma_start(T.y[:], T.x[:]).then_inc(T.sem.seeded, 16)

    g.wait_ge(T.sem.loaded, 16)
    g.remote_dma(T.land[:], T.mine[:], T.sem.arrived, T.sem.sent, pid, rid, mask)

    g.wait_ge(T.sem.arrived, n_eng)
    g.wait_ge(T.sem.seeded, 16)
    g.dma_start(T.y[:], T.land[:], accum_op=AluOpType.add).then_inc(T.sem.stored, 16)

    g.wait_ge(T.sem.stored, 16)
    g.wait_ge(T.sem.sent, n_eng)
